import numpy as np
import ml_dtypes


def mxq(x, axis, fmt="e4m3"):
    dtype, down = {"e4m3": (ml_dtypes.float8_e4m3fn, 7), "e5m2": (ml_dtypes.float8_e5m2, 14)}[fmt]
    v = np.moveaxis(np.asarray(x, np.float32).astype(ml_dtypes.bfloat16).astype(np.float64), axis, -1)
    blocks = v.reshape(v.shape[:-1] + (-1, 32))
    amax = np.abs(blocks).max(-1, keepdims=True)
    byte = np.maximum(np.where(amax > 0, np.frexp(amax)[1] - 1 + 127, 0) - down, 1)
    scale = np.exp2(byte - 127.0)
    codes = (blocks / scale).astype(np.float32).astype(dtype).astype(np.float64)
    return np.moveaxis((codes * scale).reshape(v.shape), -1, axis)


WIDE = False


def mx_kscale(k):
    if not WIDE:
        return np.ones(k)
    levels = np.array([10, -10, 5, -5, 0])
    if k % 512:
        return np.exp2(np.random.permutation(np.resize(levels, k // 32))).repeat(32)
    a = np.empty((k // 512, 16))
    for p in range(k // 512):
        a[p, :8] = np.random.permutation(np.resize(levels, 8))
        for g in range(8):
            far = levels[np.abs(levels - a[p, g]) >= 10]
            a[p, g + 8] = far[np.random.randint(len(far))]
    return np.exp2(a.ravel()).repeat(32)


def f64(x):
    return np.asarray(x).astype(np.float64)


def striped(idx):
    return np.tile(idx.reshape(-1, 16).T, (8, 1)).astype(np.uint16)


def unstriped(offs):
    return offs[:16].T.reshape(-1).astype(np.int64)


def pack_weight(w):
    k, n = w.shape
    w = f64(np.asarray(w, np.float32).astype(ml_dtypes.bfloat16)).reshape(k // 32, 32, n)
    amax = np.abs(w).max(1)
    byte = np.clip(np.where(amax > 0, np.frexp(amax)[1] - 1 + 127 - 7, 1), 1, 254)
    scaled = (w * np.exp2(127.0 - byte)[:, None, :]).reshape(k, n).astype(np.float32)
    words = np.ascontiguousarray(scaled.reshape(k // 512, 128, 4, n).transpose(0, 1, 3, 2)).astype(ml_dtypes.float8_e4m3fn).view(np.uint8)
    return words, np.ascontiguousarray(byte.astype(np.uint8).reshape(k // 512, 16, n))


def unpack_weight(words, scales):
    g, p, n, _ = words.shape
    vals = np.ascontiguousarray(words).view(ml_dtypes.float8_e4m3fn).astype(np.float64) * np.repeat(np.exp2(scales.astype(np.float64) - 127.0), 8, axis=1)[..., None]
    return vals.transpose(0, 1, 3, 2).reshape(g * 512, n)

def planes(y):
    n, m = y.shape
    v = y.astype(np.float32).astype(ml_dtypes.bfloat16).astype(np.float64).reshape(n // 32, 32, m)
    top = np.abs(v).max(1)
    byte = np.clip(np.where(top > 0, np.frexp(top)[1] - 1 + 127 - 7, 1), 1, 254)
    codes = (v * np.exp2(127.0 - byte)[:, None, :]).reshape(n, m).astype(np.float32).astype(ml_dtypes.float8_e4m3fn).view(np.uint8)
    words = codes.reshape(n // 512, 128, 4, m).transpose(0, 1, 3, 2)
    return np.ascontiguousarray(words), np.ascontiguousarray(byte.astype(np.uint8).reshape(n // 512, 16, m))


K, T, D, H = 512, 512, 3, 512
P = 2 ** 7


def setup_inputs():
    n = np.random.standard_normal
    s = mx_kscale(K)[:, None]
    u = mx_kscale(H)
    packed_xT = pack_weight(n((K, T)) * s)
    packed_w2 = pack_weight(n((H, H)) / np.sqrt(H) / u[:, None])
    return {
        "x_words": packed_xT[0],
        "x_scales": packed_xT[1],
        "w1": (n((K, H)) / np.sqrt(K) / s * u).astype(np.float32),
        "w2_words": packed_w2[0],
        "w2_scales": packed_w2[1],
        "gate": (np.tile(np.random.uniform(0.2, 1.0, (D, 1, T)) / np.sqrt(D), (1, P, 1))).astype(np.float32),
        "pos1": striped(np.random.permutation(T)),
        "pos2": striped(np.random.permutation(T)),
        "pos3": striped(np.random.permutation(T)),
    }


def reference(x_words, x_scales, w1, w2_words, w2_scales, gate, pos1, pos2, pos3):
    xq = unpack_weight(x_words, x_scales)
    h = mxq(f64(w1), 0, "e4m3").T @ xq
    z = h - (h[:, unstriped(pos1)] * f64(gate)[0, :1] + h[:, unstriped(pos2)] * f64(gate)[1, :1] + h[:, unstriped(pos3)] * f64(gate)[2, :1])
    out_0 = unpack_weight(w2_words, w2_scales).T @ mxq(z, 0, "e4m3")
    return (out_0,) + planes(out_0)

@@ -1,0 +1,225 @@
+from contextlib import ExitStack
+
+import concourse.mybir as mybir
+from concourse.masks import make_identity
+
+K, T, D, H = 512, 512, 3, 512
+FLOPS = 2 * K * H * T + 2 * H * H * T
+
+F32 = mybir.dt.float32
+BF16 = mybir.dt.bfloat16
+I32 = mybir.dt.int32
+U32 = mybir.dt.uint32
+U16 = mybir.dt.uint16
+U8 = mybir.dt.uint8
+FP8X4 = mybir.dt.float8_e4m3fn_x4
+COPY = mybir.ActivationFunctionType.Copy
+MULT = mybir.AluOpType.mult
+
+P = 128
+PACK = 4
+CHUNKS = H // P
+BLOCKS = T // P
+PIECES = ((0, 2), (2, 3), (3, 4))
+
+
+def tile_picked_wlapl_none_lo_kernel(
+    tc, x_words, x_scales, w1, w2_words, w2_scales, gate, pos1, pos2, pos3, out_0, out_1, out_2
+):
+    nc = tc.nc
+    with ExitStack() as ctx:
+        keep = ctx.enter_context(tc.tile_pool(name="keep", bufs=1))
+        psum = ctx.enter_context(tc.psum_pool(name="psum", bufs=1))
+
+        def sb(shape, dtype, name, tag=None):
+            return keep.tile(shape, dtype, name=name, tag=tag or name, align_bytes=64)
+
+        banks = [psum.tile([P, 512], F32, name="bank%d" % i) for i in range(8)]
+        acc_banks, sum_banks, back_bank = banks[0:3], banks[3:7], banks[7]
+
+        lists = [keep.tile([P, T // 16], U16, name="list%d" % d) for d in range(D)]
+        x_codes = sb([P, T], U32, "x_codes")
+        x_plane = sb([P, T], U8, "x_plane")
+        w2_raw = sb([P, H], U32, "w2_raw")
+        w2_raw_plane = sb([P, H], U8, "w2_raw_plane")
+        w2_codes = sb([P, H], U32, "w2_codes")
+        w2_plane = sb([P, H], U8, "w2_plane")
+        w1_raw = [sb([P, PACK, P], F32, "w1_raw%d" % c) for c in range(CHUNKS)]
+        gates = [sb([P, D, (b1 - b0) * P], F32, "gates%d" % b0) for b0, b1 in PIECES]
+        identity = sb([P, P], F32, "identity")
+        warm = sb([P, 8], F32, "warm")
+        y_codes = sb([P, T], U32, "y_codes")
+        y_plane = sb([P, T], U8, "y_plane")
+
+        def load_scales(queue, plane, rows):
+            for q in range(4):
+                queue.dma_start(out=plane[32 * q : 32 * q + 4, :].bitcast(I32), in_=rows[0, 4 * q : 4 * q + 4, :].bitcast(I32))
+
+        def load_words(codes, words):
+            nc.sync.dma_start(out=codes[:].bitcast(I32), in_=words[0].rearrange("p n t -> p (n t)").bitcast(I32))
+
+        def load_w1(c):
+            nc.sync.dma_start(out=w1_raw[c][:], in_=w1[:, c * P : (c + 1) * P].rearrange("(p j) m -> p j m", j=PACK))
+
+        def load_gates(i):
+            b0, b1 = PIECES[i]
+            nc.sync.dma_start(out=gates[i][:], in_=gate[:, :, b0 * P : b1 * P].rearrange("d p v -> p d v"))
+
+        nc.vector.memset(x_plane[:].bitcast(I32), 0)
+        nc.gpsimd.memset(w2_raw_plane[:].bitcast(I32), 0)
+        load_scales(nc.scalar, x_plane, x_scales)
+        load_w1(0)
+        load_words(x_codes, x_words)
+        nc.sync.dma_start(lists[0][:], pos1)
+        load_gates(0)
+        load_w1(1)
+        nc.sync.dma_start(lists[1][:], pos2)
+        nc.sync.dma_start(lists[2][:], pos3)
+        load_words(w2_raw, w2_words)
+        load_w1(2)
+        load_w1(3)
+        load_scales(nc.sync, w2_raw_plane, w2_scales)
+        load_gates(1)
+        load_gates(2)
+        make_identity(nc, identity[:])
+        nc.vector.memset(warm[:], 0.0)
+        nc.scalar.activation(out=warm[:, 0:1], in_=warm[:, 1:2], func=COPY, scale=-1.0)
+
+        h, h_neg = [], []
+
+        def first_layer(c):
+            grouped = sb([P, P, PACK], BF16, "w1_bf%d" % c)
+            source = w1_raw[c][:].rearrange("p j m -> p m j")
+            if c == 0:
+                nc.vector.tensor_copy(out=grouped[:], in_=source)
+            else:
+                nc.scalar.copy(out=grouped[:], in_=source)
+            codes = sb([P, P], U32, "w1_codes%d" % c)
+            plane = sb([P, P], U8, "w1_plane%d" % c)
+            nc.vector.quantize_mx(out=codes[:].bitcast(FP8X4), scales=plane[:], in_=grouped[:].rearrange("p m j -> p (m j)"))
+            bank = acc_banks[c % 3]
+            nc.tensor.matmul_mx(
+                out=bank[:], lhsT=codes[:].bitcast(FP8X4), lhsT_scale=plane[:],
+                rhs=x_codes[:].bitcast(FP8X4), rhs_scale=x_plane[:], start=True, stop=True,
+            )
+            h.append(sb([P, T], F32, "h%d" % c))
+            h_neg.append(sb([P, T], F32, "h_neg%d" % c))
+            nc.scalar.copy(out=h[c][:], in_=bank[:])
+            nc.scalar.activation(out=h_neg[c][:], in_=bank[:], func=COPY, scale=-1.0)
+
+        def deal_w2():
+            nc.vector.tensor_copy(
+                out=w2_codes[:].bitcast(I32).rearrange("p (t m) -> p t m", t=PACK),
+                in_=w2_raw[:].bitcast(I32).rearrange("p (m t) -> p t m", t=PACK),
+            )
+            nc.vector.tensor_copy(
+                out=w2_plane[:].rearrange("p (t m) -> p t m", t=PACK),
+                in_=w2_raw_plane[:].rearrange("p (m t) -> p t m", t=PACK),
+            )
+
+        def sum_bank(b, c):
+            if b == BLOCKS - 1 and c == CHUNKS - 1:
+                return sum_banks[0]
+            return sum_banks[b]
+
+        def add_turned(b, c, rows, start, stop):
+            nc.tensor.matmul(
+                out=sum_bank(b, c)[:, c * P : (c + 1) * P], lhsT=rows, rhs=identity[:],
+                is_transpose=True, start=start, stop=stop,
+            )
+
+        def gather(i, c, after=None):
+            b0, b1 = PIECES[i]
+            terms = sb([P, D, (b1 - b0) * P], F32, "terms%d_%d" % (i, c), after)
+            for d in range(D):
+                term = terms[:, d, :]
+                offsets = lists[d][:, b0 * P // 16 : b1 * P // 16]
+                nc.vector.tensor_tensor(term, h[c][:].indirect(offsets), gates[i][:, d, :], MULT)
+                for b in range(b0, b1):
+                    if d == D - 1:
+                        add_turned(b, c, h_neg[c][:, b * P : (b + 1) * P], False, False)
+                    add_turned(b, c, term[:, (b - b0) * P : (b - b0 + 1) * P], d == 0, d == D - 1)
+
+        z_rows = [sb([P, 2, P, 2], BF16, "z_rows%d" % b) for b in range(BLOCKS)]
+
+        def round_z(b, c0, c1):
+            rows = slice(32 * c0, 32 * c1)
+            nc.scalar.activation(
+                out=z_rows[b][:, :, rows, :],
+                in_=sum_bank(b, c0)[:].rearrange("v (p u e) -> v u p e", u=2, e=2)[:, :, rows, :],
+                func=COPY, scale=-1.0,
+            )
+
+        results = {}
+
+        def second_layer(b):
+            words = z_rows[b][:].rearrange("v u p e -> v (u p e)").bitcast(F32)
+            for u in range(2):
+                nc.tensor.transpose(back_bank[:, u * P : (u + 1) * P], words[:, u * P : (u + 1) * P], identity[:])
+            z_grouped = sb([P, P * PACK], BF16, "z_grouped%d" % b)
+            nc.scalar.copy(
+                out=z_grouped[:].bitcast(F32).rearrange("p (v u) -> p v u", u=2),
+                in_=back_bank[:, 0 : 2 * P].rearrange("p (u v) -> p v u", u=2),
+            )
+            codes = sb([P, P], U32, "z_codes%d" % b)
+            plane = sb([P, P], U8, "z_plane%d" % b)
+            nc.vector.quantize_mx(out=codes[:].bitcast(FP8X4), scales=plane[:], in_=z_grouped[:])
+            bank = acc_banks[(b + 1) % 3]
+            for t in range(PACK):
+                m = slice(t * P, (t + 1) * P)
+                nc.tensor.matmul_mx(
+                    out=bank[:, m], lhsT=w2_codes[:, m].bitcast(FP8X4), lhsT_scale=w2_plane[:, m],
+                    rhs=codes[:].bitcast(FP8X4), rhs_scale=plane[:], start=True, stop=True,
+                )
+            y_grouped = sb([P, P, PACK], BF16, "y_grouped%d" % b)
+            turned = bank[:].rearrange("p (t v) -> p v t", t=PACK)
+            if b >= BLOCKS - 2:
+                nc.vector.tensor_copy(out=y_grouped[:], in_=turned)
+            else:
+                nc.scalar.copy(out=y_grouped[:], in_=turned)
+            y = sb([P, PACK, P], F32, "y%d" % b)
+            nc.scalar.copy(out=y[:].rearrange("p t v -> p (t v)"), in_=bank[:])
+            results[b] = (y, y_grouped)
+
+        def finish(b):
+            cols = slice(b * P, (b + 1) * P)
+            y, y_grouped = results[b]
+            nc.vector.quantize_mx(
+                out=y_codes[:, cols].bitcast(FP8X4), scales=y_plane[:, cols],
+                in_=y_grouped[:].rearrange("p v t -> p (v t)"),
+            )
+            nc.sync.dma_start(out=out_0.rearrange("(p t) v -> p t v", t=PACK)[:, :, cols], in_=y[:])
+            nc.sync.dma_start(
+                out=out_1[0].rearrange("p n t -> p (n t)").bitcast(I32)[:, cols], in_=y_codes[:, cols].bitcast(I32)
+            )
+
+        first_layer(0)
+        for c in range(CHUNKS):
+            if c + 1 < CHUNKS:
+                first_layer(c + 1)
+            gather(0, c)
+            if c == 2:
+                deal_w2()
+        round_z(0, 0, CHUNKS)
+        round_z(1, 0, CHUNKS)
+        for c in range(CHUNKS - 1):
+            gather(1, c)
+        second_layer(0)
+        second_layer(1)
+        gather(1, 3, "z_grouped0")
+        round_z(2, 0, CHUNKS)
+        gather(2, 0, "z_grouped1")
+        finish(0)
+        gather(2, 1, "y_grouped0")
+        finish(1)
+        gather(2, 2, "y_grouped1")
+        round_z(3, 0, CHUNKS - 1)
+        second_layer(2)
+        gather(2, 3, "z_grouped2")
+        round_z(3, CHUNKS - 1, CHUNKS)
+        finish(2)
+        second_layer(3)
+        finish(3)
+        for q in range(4):
+            queue = nc.scalar if q % 2 else nc.sync
+            queue.dma_start(out=out_2[0, 4 * q : 4 * q + 4, :].bitcast(I32), in_=y_plane[32 * q : 32 * q + 4, :].bitcast(I32))

@@ -35,7 +35,7 @@ def tile_picked_wlapl_none_lo_kernel(
             return keep.tile(shape, dtype, name=name, tag=tag or name, align_bytes=64)
 
         banks = [psum.tile([P, 512], F32, name="bank%d" % i) for i in range(8)]
-        acc_banks, sum_banks, back_bank = banks[0:3], banks[3:7], banks[7]
+        acc_banks, sum_banks, back_banks = banks[0:3], banks[3:6], banks[6:8]
 
         lists = [keep.tile([P, T // 16], U16, name="list%d" % d) for d in range(D)]
         x_codes = sb([P, T], U32, "x_codes")
@@ -44,7 +44,8 @@ def tile_picked_wlapl_none_lo_kernel(
         w2_raw_plane = sb([P, H], U8, "w2_raw_plane")
         w2_codes = sb([P, H], U32, "w2_codes")
         w2_plane = sb([P, H], U8, "w2_plane")
-        w1_raw = [sb([P, PACK, P], F32, "w1_raw%d" % c) for c in range(CHUNKS)]
+        w1_raw = {}
+        gates_raw = {}
         gates = [sb([P, D, (b1 - b0) * P], F32, "gates%d" % b0) for b0, b1 in PIECES]
         identity = sb([P, P], F32, "identity")
         warm = sb([P, 8], F32, "warm")
@@ -58,38 +59,49 @@ def tile_picked_wlapl_none_lo_kernel(
         def load_words(codes, words):
             nc.sync.dma_start(out=codes[:].bitcast(I32), in_=words[0].rearrange("p n t -> p (n t)").bitcast(I32))
 
-        def load_w1(c):
-            nc.sync.dma_start(out=w1_raw[c][:], in_=w1[:, c * P : (c + 1) * P].rearrange("(p j) m -> p j m", j=PACK))
+        def load_w1(c0, c1):
+            raw = sb([P, PACK, (c1 - c0) * P], F32, "w1_raw%d" % c0)
+            nc.sync.dma_start(out=raw[:], in_=w1[:, c0 * P : c1 * P].rearrange("(p j) m -> p j m", j=PACK))
+            for c in range(c0, c1):
+                w1_raw[c] = raw[:, :, (c - c0) * P : (c - c0 + 1) * P]
 
-        def load_gates(i):
-            b0, b1 = PIECES[i]
-            nc.sync.dma_start(out=gates[i][:], in_=gate[:, :, b0 * P : b1 * P].rearrange("d p v -> p d v"))
+        def load_gates(b0, b1):
+            raw = sb([P, D, (b1 - b0) * P], F32, "gates_raw%d" % b0)
+            nc.sync.dma_start(out=raw[:], in_=gate[:, :, b0 * P : b1 * P].rearrange("d p v -> p d v"))
+            gates_raw[b0] = raw
 
-        nc.vector.memset(x_plane[:].bitcast(I32), 0)
+        def negate_gates(i):
+            if i == 0:
+                for d in range(D):
+                    nc.scalar.activation(out=gates[0][:, d, :], in_=gates_raw[0][:, d, :], func=COPY, scale=-1.0)
+            else:
+                nc.scalar.activation(
+                    out=gates[i][:], in_=gates_raw[2][:, :, (i - 1) * P : i * P], func=COPY, scale=-1.0
+                )
+
+        nc.gpsimd.memset(x_plane[:].bitcast(I32), 0)
         nc.gpsimd.memset(w2_raw_plane[:].bitcast(I32), 0)
-        load_scales(nc.scalar, x_plane, x_scales)
-        load_w1(0)
+        make_identity(nc, identity[:])
+        load_scales(nc.gpsimd, w2_raw_plane, w2_scales)
+        load_w1(0, 1)
+        load_scales(nc.sync, x_plane, x_scales)
         load_words(x_codes, x_words)
         nc.sync.dma_start(lists[0][:], pos1)
-        load_gates(0)
-        load_w1(1)
+        load_w1(1, 2)
+        load_gates(0, 2)
+        load_words(w2_raw, w2_words)
         nc.sync.dma_start(lists[1][:], pos2)
         nc.sync.dma_start(lists[2][:], pos3)
-        load_words(w2_raw, w2_words)
-        load_w1(2)
-        load_w1(3)
-        load_scales(nc.sync, w2_raw_plane, w2_scales)
-        load_gates(1)
-        load_gates(2)
-        make_identity(nc, identity[:])
+        load_w1(2, 4)
+        load_gates(2, 4)
         nc.vector.memset(warm[:], 0.0)
         nc.scalar.activation(out=warm[:, 0:1], in_=warm[:, 1:2], func=COPY, scale=-1.0)
 
-        h, h_neg = [], []
+        h, made = [], {}
 
         def first_layer(c):
             grouped = sb([P, P, PACK], BF16, "w1_bf%d" % c)
-            source = w1_raw[c][:].rearrange("p j m -> p m j")
+            source = w1_raw[c].rearrange("p j m -> p m j")
             if c == 0:
                 nc.vector.tensor_copy(out=grouped[:], in_=source)
             else:
@@ -97,30 +109,36 @@ def tile_picked_wlapl_none_lo_kernel(
             codes = sb([P, P], U32, "w1_codes%d" % c)
             plane = sb([P, P], U8, "w1_plane%d" % c)
             nc.vector.quantize_mx(out=codes[:].bitcast(FP8X4), scales=plane[:], in_=grouped[:].rearrange("p m j -> p (m j)"))
-            bank = acc_banks[c % 3]
-            nc.tensor.matmul_mx(
-                out=bank[:], lhsT=codes[:].bitcast(FP8X4), lhsT_scale=plane[:],
-                rhs=x_codes[:].bitcast(FP8X4), rhs_scale=x_plane[:], start=True, stop=True,
-            )
             h.append(sb([P, T], F32, "h%d" % c))
-            h_neg.append(sb([P, T], F32, "h_neg%d" % c))
-            nc.scalar.copy(out=h[c][:], in_=bank[:])
-            nc.scalar.activation(out=h_neg[c][:], in_=bank[:], func=COPY, scale=-1.0)
+            parts = 2 if c == 0 else 1
+            for part in range(parts):
+                cols = slice(part * T // parts, (part + 1) * T // parts)
+                bank = acc_banks[(c + 2 * part) % 3]
+                nc.tensor.matmul_mx(
+                    out=bank[:, cols], lhsT=codes[:].bitcast(FP8X4), lhsT_scale=plane[:],
+                    rhs=x_codes[:, cols].bitcast(FP8X4), rhs_scale=x_plane[:, cols], start=True, stop=True,
+                )
+                if part == 0:
+                    nc.scalar.copy(out=h[c][:, cols], in_=bank[:, cols])
+                else:
+                    nc.vector.tensor_copy(out=h[c][:, cols], in_=bank[:, cols])
 
         def deal_w2():
             nc.vector.tensor_copy(
-                out=w2_codes[:].bitcast(I32).rearrange("p (t m) -> p t m", t=PACK),
-                in_=w2_raw[:].bitcast(I32).rearrange("p (m t) -> p t m", t=PACK),
+                out=w2_codes[:].bitcast(I32).rearrange("p (t c i) -> p c t i", t=PACK, i=4),
+                in_=w2_raw[:].bitcast(I32).rearrange("p (c i t) -> p c t i", t=PACK, i=4),
             )
+
+        def deal_w2_plane():
             nc.vector.tensor_copy(
-                out=w2_plane[:].rearrange("p (t m) -> p t m", t=PACK),
-                in_=w2_raw_plane[:].rearrange("p (m t) -> p t m", t=PACK),
+                out=w2_plane[:].rearrange("p (t c i) -> p c t i", t=PACK, i=16),
+                in_=w2_raw_plane[:].rearrange("p (c i t) -> p c t i", t=PACK, i=16),
             )
 
         def sum_bank(b, c):
             if b == BLOCKS - 1 and c == CHUNKS - 1:
-                return sum_banks[0]
-            return sum_banks[b]
+                return sum_banks[1]
+            return sum_banks[b % 3]
 
         def add_turned(b, c, rows, start, stop):
             nc.tensor.matmul(
@@ -128,31 +146,35 @@ def tile_picked_wlapl_none_lo_kernel(
                 is_transpose=True, start=start, stop=stop,
             )
 
-        def gather(i, c, after=None):
+        def gather(i, c, after=None, terms=None):
             b0, b1 = PIECES[i]
-            terms = sb([P, D, (b1 - b0) * P], F32, "terms%d_%d" % (i, c), after)
+            if terms is None:
+                terms = sb([P, D, (b1 - b0) * P], F32, "terms%d_%d" % (i, c), after)
+            made[i, c] = terms
+            for b in range(b0, b1):
+                add_turned(b, c, h[c][:, b * P : (b + 1) * P], True, False)
             for d in range(D):
                 term = terms[:, d, :]
                 offsets = lists[d][:, b0 * P // 16 : b1 * P // 16]
                 nc.vector.tensor_tensor(term, h[c][:].indirect(offsets), gates[i][:, d, :], MULT)
                 for b in range(b0, b1):
-                    if d == D - 1:
-                        add_turned(b, c, h_neg[c][:, b * P : (b + 1) * P], False, False)
-                    add_turned(b, c, term[:, (b - b0) * P : (b - b0 + 1) * P], d == 0, d == D - 1)
+                    add_turned(b, c, term[:, (b - b0) * P : (b - b0 + 1) * P], False, d == D - 1)
 
         z_rows = [sb([P, 2, P, 2], BF16, "z_rows%d" % b) for b in range(BLOCKS)]
 
         def round_z(b, c0, c1):
             rows = slice(32 * c0, 32 * c1)
-            nc.scalar.activation(
+            nc.scalar.copy(
                 out=z_rows[b][:, :, rows, :],
                 in_=sum_bank(b, c0)[:].rearrange("v (p u e) -> v u p e", u=2, e=2)[:, :, rows, :],
-                func=COPY, scale=-1.0,
             )
 
         results = {}
 
-        def second_layer(b):
+        grouped_z = {}
+
+        def turn_back(b):
+            back_bank = back_banks[b % 2]
             words = z_rows[b][:].rearrange("v u p e -> v (u p e)").bitcast(F32)
             for u in range(2):
                 nc.tensor.transpose(back_bank[:, u * P : (u + 1) * P], words[:, u * P : (u + 1) * P], identity[:])
@@ -161,24 +183,38 @@ def tile_picked_wlapl_none_lo_kernel(
                 out=z_grouped[:].bitcast(F32).rearrange("p (v u) -> p v u", u=2),
                 in_=back_bank[:, 0 : 2 * P].rearrange("p (u v) -> p v u", u=2),
             )
+            grouped_z[b] = z_grouped
+
+        def second_layer(b):
+            z_grouped = grouped_z[b]
             codes = sb([P, P], U32, "z_codes%d" % b)
             plane = sb([P, P], U8, "z_plane%d" % b)
             nc.vector.quantize_mx(out=codes[:].bitcast(FP8X4), scales=plane[:], in_=z_grouped[:])
+            last = b == BLOCKS - 1
             bank = acc_banks[(b + 1) % 3]
+            y = sb([P, PACK, P], F32, "y%d" % b)
+            flat = y[:].rearrange("p t v -> p (t v)")
             for t in range(PACK):
                 m = slice(t * P, (t + 1) * P)
+                target = acc_banks[(b + 2) % 3] if last and t >= 2 else bank
                 nc.tensor.matmul_mx(
-                    out=bank[:, m], lhsT=w2_codes[:, m].bitcast(FP8X4), lhsT_scale=w2_plane[:, m],
+                    out=target[:, m], lhsT=w2_codes[:, m].bitcast(FP8X4), lhsT_scale=w2_plane[:, m],
                     rhs=codes[:].bitcast(FP8X4), rhs_scale=plane[:], start=True, stop=True,
                 )
             y_grouped = sb([P, P, PACK], BF16, "y_grouped%d" % b)
             turned = bank[:].rearrange("p (t v) -> p v t", t=PACK)
-            if b >= BLOCKS - 2:
-                nc.vector.tensor_copy(out=y_grouped[:], in_=turned)
+            if last:
+                other = acc_banks[(b + 2) % 3]
+                nc.scalar.copy(out=y_grouped[:, :, 0:2], in_=turned[:, :, 0:2])
+                nc.vector.tensor_copy(out=y_grouped[:, :, 2:4], in_=other[:].rearrange("p (t v) -> p v t", t=PACK)[:, :, 2:4])
+                nc.scalar.copy(out=flat[:, 0 : 2 * P], in_=bank[:, 0 : 2 * P])
+                nc.scalar.copy(out=flat[:, 2 * P : 4 * P], in_=other[:, 2 * P : 4 * P])
             else:
-                nc.scalar.copy(out=y_grouped[:], in_=turned)
-            y = sb([P, PACK, P], F32, "y%d" % b)
-            nc.scalar.copy(out=y[:].rearrange("p t v -> p (t v)"), in_=bank[:])
+                if b == BLOCKS - 2:
+                    nc.vector.tensor_copy(out=y_grouped[:], in_=turned)
+                else:
+                    nc.scalar.copy(out=y_grouped[:], in_=turned)
+                nc.scalar.copy(out=flat, in_=bank[:])
             results[b] = (y, y_grouped)
 
         def finish(b):
@@ -188,35 +224,52 @@ def tile_picked_wlapl_none_lo_kernel(
                 out=y_codes[:, cols].bitcast(FP8X4), scales=y_plane[:, cols],
                 in_=y_grouped[:].rearrange("p v t -> p (v t)"),
             )
-            nc.sync.dma_start(out=out_0.rearrange("(p t) v -> p t v", t=PACK)[:, :, cols], in_=y[:])
+            rows = out_0.rearrange("(p t) v -> p t v", t=PACK)
+            if b == BLOCKS - 1:
+                nc.sync.dma_start(out=rows[:, 0:2, cols], in_=y[:, 0:2, :])
+                nc.scalar.dma_start(out=rows[:, 2:4, cols], in_=y[:, 2:4, :])
+            else:
+                nc.sync.dma_start(out=rows[:, :, cols], in_=y[:])
             nc.sync.dma_start(
                 out=out_1[0].rearrange("p n t -> p (n t)").bitcast(I32)[:, cols], in_=y_codes[:, cols].bitcast(I32)
             )
 
         first_layer(0)
-        for c in range(CHUNKS):
-            if c + 1 < CHUNKS:
-                first_layer(c + 1)
-            gather(0, c)
-            if c == 2:
-                deal_w2()
+        negate_gates(0)
+        first_layer(1)
+        deal_w2()
+        gather(0, 0)
+        first_layer(2)
+        gather(0, 1, "w1_bf2")
+        first_layer(3)
+        gather(0, 2, "w1_bf3")
+        negate_gates(1)
+        negate_gates(2)
+        gather(0, 3)
+        deal_w2_plane()
         round_z(0, 0, CHUNKS)
         round_z(1, 0, CHUNKS)
-        for c in range(CHUNKS - 1):
-            gather(1, c)
+        held = sb([P, CHUNKS, D, P], F32, "held", "w1_bf3")
+        gather(1, 0, None, held[:, 0, :, :])
+        gather(1, 1, None, held[:, 1, :, :])
+        turn_back(0)
+        gather(1, 2, None, held[:, 2, :, :])
+        turn_back(1)
+        gather(1, 3, None, held[:, 3, :, :])
         second_layer(0)
-        second_layer(1)
-        gather(1, 3, "z_grouped0")
         round_z(2, 0, CHUNKS)
-        gather(2, 0, "z_grouped1")
+        gather(2, 0, "z_grouped0")
+        second_layer(1)
+        gather(2, 1, "z_grouped1")
+        turn_back(2)
         finish(0)
-        gather(2, 1, "y_grouped0")
+        gather(2, 2, "y_grouped0")
         finish(1)
-        gather(2, 2, "y_grouped1")
         round_z(3, 0, CHUNKS - 1)
-        second_layer(2)
-        gather(2, 3, "z_grouped2")
+        gather(2, 3, "y_grouped1")
         round_z(3, CHUNKS - 1, CHUNKS)
+        second_layer(2)
+        turn_back(3)
         finish(2)
         second_layer(3)
         finish(3)

@@ -20,7 +20,6 @@ P = 128
 PACK = 4
 CHUNKS = H // P
 BLOCKS = T // P
-PIECES = ((0, 2), (2, 3), (3, 4))
 
 
 def tile_picked_wlapl_none_lo_kernel(
@@ -45,15 +44,14 @@ def tile_picked_wlapl_none_lo_kernel(
         w2_codes = sb([P, H], U32, "w2_codes")
         w2_plane = sb([P, H], U8, "w2_plane")
         w1_raw = {}
-        gates_raw = {}
-        gates = [sb([P, D, (b1 - b0) * P], F32, "gates%d" % b0) for b0, b1 in PIECES]
+        gates = [sb([P, T], F32, "gates%d" % d) for d in range(D)]
         identity = sb([P, P], F32, "identity")
         warm = sb([P, 8], F32, "warm")
         y_codes = sb([P, T], U32, "y_codes")
         y_plane = sb([P, T], U8, "y_plane")
 
-        def load_scales(queue, plane, rows):
-            for q in range(4):
+        def load_scales(queue, plane, rows, quadrants=range(4)):
+            for q in quadrants:
                 queue.dma_start(out=plane[32 * q : 32 * q + 4, :].bitcast(I32), in_=rows[0, 4 * q : 4 * q + 4, :].bitcast(I32))
 
         def load_words(codes, words):
@@ -65,35 +63,31 @@ def tile_picked_wlapl_none_lo_kernel(
             for c in range(c0, c1):
                 w1_raw[c] = raw[:, :, (c - c0) * P : (c - c0 + 1) * P]
 
-        def load_gates(b0, b1):
-            raw = sb([P, D, (b1 - b0) * P], F32, "gates_raw%d" % b0)
-            nc.sync.dma_start(out=raw[:], in_=gate[:, :, b0 * P : b1 * P].rearrange("d p v -> p d v"))
-            gates_raw[b0] = raw
+        def load_gates(d0, d1, b0, b1):
+            raw = sb([P, d1 - d0, (b1 - b0) * P], F32, "gates_raw%d_%d" % (d0, b0))
+            nc.sync.dma_start(out=raw[:], in_=gate[d0:d1, :, b0 * P : b1 * P].rearrange("d p v -> p d v"))
+            return raw
 
-        def negate_gates(i):
-            if i == 0:
-                for d in range(D):
-                    nc.scalar.activation(out=gates[0][:, d, :], in_=gates_raw[0][:, d, :], func=COPY, scale=-1.0)
-            else:
-                nc.scalar.activation(
-                    out=gates[i][:], in_=gates_raw[2][:, :, (i - 1) * P : i * P], func=COPY, scale=-1.0
-                )
+        def negate_gates(raw, d0, d1, b0, b1):
+            for d in range(d0, d1):
+                nc.scalar.activation(out=gates[d][:, b0 * P : b1 * P], in_=raw[:, d - d0, :], func=COPY, scale=-1.0)
 
         nc.gpsimd.memset(x_plane[:].bitcast(I32), 0)
         nc.gpsimd.memset(w2_raw_plane[:].bitcast(I32), 0)
+        load_scales(nc.gpsimd, w2_raw_plane, w2_scales, (0, 1))
         make_identity(nc, identity[:])
-        load_scales(nc.gpsimd, w2_raw_plane, w2_scales)
         load_w1(0, 1)
         load_scales(nc.sync, x_plane, x_scales)
         load_words(x_codes, x_words)
-        nc.sync.dma_start(lists[0][:], pos1)
         load_w1(1, 2)
-        load_gates(0, 2)
+        first = load_gates(0, 3, 0, 2)
         load_words(w2_raw, w2_words)
-        nc.sync.dma_start(lists[1][:], pos2)
-        nc.sync.dma_start(lists[2][:], pos3)
-        load_w1(2, 4)
-        load_gates(2, 4)
+        load_scales(nc.sync, w2_raw_plane, w2_scales, (2, 3))
+        for d, pos in enumerate((pos1, pos2, pos3)):
+            nc.sync.dma_start(lists[d][:], pos)
+        load_w1(2, 3)
+        load_w1(3, 4)
+        rest = load_gates(0, 3, 2, 4)
         nc.vector.memset(warm[:], 0.0)
         nc.scalar.activation(out=warm[:, 0:1], in_=warm[:, 1:2], func=COPY, scale=-1.0)
 
@@ -146,19 +140,18 @@ def tile_picked_wlapl_none_lo_kernel(
                 is_transpose=True, start=start, stop=stop,
             )
 
-        def gather(i, c, after=None, terms=None):
-            b0, b1 = PIECES[i]
-            if terms is None:
-                terms = sb([P, D, (b1 - b0) * P], F32, "terms%d_%d" % (i, c), after)
-            made[i, c] = terms
+        def gather(b0, b1, c, terms):
             for b in range(b0, b1):
                 add_turned(b, c, h[c][:, b * P : (b + 1) * P], True, False)
             for d in range(D):
-                term = terms[:, d, :]
                 offsets = lists[d][:, b0 * P // 16 : b1 * P // 16]
-                nc.vector.tensor_tensor(term, h[c][:].indirect(offsets), gates[i][:, d, :], MULT)
+                nc.vector.tensor_tensor(terms[d], h[c][:].indirect(offsets), gates[d][:, b0 * P : b1 * P], MULT)
                 for b in range(b0, b1):
-                    add_turned(b, c, term[:, (b - b0) * P : (b - b0 + 1) * P], False, d == D - 1)
+                    add_turned(b, c, terms[d][:, (b - b0) * P : (b - b0 + 1) * P], False, d == D - 1)
+
+        def room(count, width, name, tag=None):
+            tile = sb([P, count, width], F32, name, tag)
+            return [tile[:, i, :] for i in range(count)]
 
         z_rows = [sb([P, 2, P, 2], BF16, "z_rows%d" % b) for b in range(BLOCKS)]
 
@@ -215,61 +208,61 @@ def tile_picked_wlapl_none_lo_kernel(
                 else:
                     nc.scalar.copy(out=y_grouped[:], in_=turned)
                 nc.scalar.copy(out=flat, in_=bank[:])
-            results[b] = (y, y_grouped)
+            rows = out_0.rearrange("(p t) v -> p t v", t=PACK)[:, :, b * P : (b + 1) * P]
+            if last:
+                nc.sync.dma_start(out=rows[:, 0:2, :], in_=y[:, 0:2, :])
+                nc.scalar.dma_start(out=rows[:, 2:4, :], in_=y[:, 2:4, :])
+            else:
+                nc.sync.dma_start(out=rows, in_=y[:])
+            results[b] = y_grouped
 
         def finish(b):
             cols = slice(b * P, (b + 1) * P)
-            y, y_grouped = results[b]
+            y_grouped = results[b]
             nc.vector.quantize_mx(
                 out=y_codes[:, cols].bitcast(FP8X4), scales=y_plane[:, cols],
                 in_=y_grouped[:].rearrange("p v t -> p (v t)"),
             )
-            rows = out_0.rearrange("(p t) v -> p t v", t=PACK)
-            if b == BLOCKS - 1:
-                nc.sync.dma_start(out=rows[:, 0:2, cols], in_=y[:, 0:2, :])
-                nc.scalar.dma_start(out=rows[:, 2:4, cols], in_=y[:, 2:4, :])
-            else:
-                nc.sync.dma_start(out=rows[:, :, cols], in_=y[:])
             nc.sync.dma_start(
                 out=out_1[0].rearrange("p n t -> p (n t)").bitcast(I32)[:, cols], in_=y_codes[:, cols].bitcast(I32)
             )
 
         first_layer(0)
-        negate_gates(0)
+        negate_gates(first, 0, 3, 0, 2)
         first_layer(1)
         deal_w2()
-        gather(0, 0)
-        first_layer(2)
-        gather(0, 1, "w1_bf2")
-        first_layer(3)
-        gather(0, 2, "w1_bf3")
-        negate_gates(1)
-        negate_gates(2)
-        gather(0, 3)
         deal_w2_plane()
+        gather(0, 2, 0, room(D, 2 * P, "terms_a"))
+        first_layer(2)
+        gather(0, 2, 1, room(D, 2 * P, "terms_c", "w1_bf2"))
+        first_layer(3)
+        gather(0, 2, 2, room(D, 2 * P, "terms_d", "w1_bf3"))
+        negate_gates(rest, 0, 3, 2, 4)
+        gather(0, 2, 3, room(D, 2 * P, "terms_e"))
         round_z(0, 0, CHUNKS)
         round_z(1, 0, CHUNKS)
-        held = sb([P, CHUNKS, D, P], F32, "held", "w1_bf3")
-        gather(1, 0, None, held[:, 0, :, :])
-        gather(1, 1, None, held[:, 1, :, :])
+        held = room(CHUNKS * D, P, "held", "w1_bf3")
+        gather(2, 3, 0, held[0:3])
+        gather(2, 3, 1, held[3:6])
         turn_back(0)
-        gather(1, 2, None, held[:, 2, :, :])
+        gather(2, 3, 2, held[6:9])
         turn_back(1)
-        gather(1, 3, None, held[:, 3, :, :])
+        gather(2, 3, 3, held[9:12])
         second_layer(0)
         round_z(2, 0, CHUNKS)
-        gather(2, 0, "z_grouped0")
+        gather(3, 4, 0, room(D, P, "terms_f", "z_grouped0"))
         second_layer(1)
-        gather(2, 1, "z_grouped1")
+        late = room(3 * D, P, "late", "z_grouped1")
+        gather(3, 4, 1, late[0:3])
         turn_back(2)
-        finish(0)
-        gather(2, 2, "y_grouped0")
-        finish(1)
+        gather(3, 4, 2, late[3:6])
         round_z(3, 0, CHUNKS - 1)
-        gather(2, 3, "y_grouped1")
+        gather(3, 4, 3, late[6:9])
         round_z(3, CHUNKS - 1, CHUNKS)
         second_layer(2)
         turn_back(3)
+        finish(0)
+        finish(1)
         finish(2)
         second_layer(3)
         finish(3)

from contextlib import ExitStack

import concourse.mybir as mybir
from concourse.masks import make_identity

K, T, D, H = 512, 512, 3, 512
FLOPS = 2 * K * H * T + 2 * H * H * T

F32 = mybir.dt.float32
BF16 = mybir.dt.bfloat16
I32 = mybir.dt.int32
U32 = mybir.dt.uint32
U16 = mybir.dt.uint16
U8 = mybir.dt.uint8
FP8X4 = mybir.dt.float8_e4m3fn_x4
COPY = mybir.ActivationFunctionType.Copy
MULT = mybir.AluOpType.mult

P = 128
PACK = 4
CHUNKS = H // P
BLOCKS = T // P


def tile_picked_wlapl_none_lo_kernel(
    tc, x_words, x_scales, w1, w2_words, w2_scales, gate, pos1, pos2, pos3, out_0, out_1, out_2
):
    nc = tc.nc
    with ExitStack() as ctx:
        keep = ctx.enter_context(tc.tile_pool(name="keep", bufs=1))
        psum = ctx.enter_context(tc.psum_pool(name="psum", bufs=1))

        def sb(shape, dtype, name, tag=None):
            return keep.tile(shape, dtype, name=name, tag=tag or name, align_bytes=64)

        banks = [psum.tile([P, 512], F32, name="bank%d" % i) for i in range(8)]
        acc_banks, sum_banks, back_banks = banks[0:3], banks[3:6], banks[6:8]

        lists = [keep.tile([P, T // 16], U16, name="list%d" % d) for d in range(D)]
        x_codes = sb([P, T], U32, "x_codes")
        x_plane = sb([P, T], U8, "x_plane")
        w2_raw = sb([P, H], U32, "w2_raw")
        w2_raw_plane = sb([P, H], U8, "w2_raw_plane")
        w2_codes = sb([P, H], U32, "w2_codes")
        w2_plane = sb([P, H], U8, "w2_plane")
        w1_raw = {}
        gates = [sb([P, T], F32, "gates%d" % d) for d in range(D)]
        identity = sb([P, P], F32, "identity")
        warm = sb([P, 8], F32, "warm")
        y_codes = sb([P, T], U32, "y_codes")
        y_plane = sb([P, T], U8, "y_plane")

        def load_scales(queue, plane, rows, quadrants=range(4)):
            for q in quadrants:
                queue.dma_start(out=plane[32 * q : 32 * q + 4, :].bitcast(I32), in_=rows[0, 4 * q : 4 * q + 4, :].bitcast(I32))

        def load_words(codes, words):
            nc.sync.dma_start(out=codes[:].bitcast(I32), in_=words[0].rearrange("p n t -> p (n t)").bitcast(I32))

        def load_w1(c0, c1):
            raw = sb([P, PACK, (c1 - c0) * P], F32, "w1_raw%d" % c0)
            nc.sync.dma_start(out=raw[:], in_=w1[:, c0 * P : c1 * P].rearrange("(p j) m -> p j m", j=PACK))
            for c in range(c0, c1):
                w1_raw[c] = raw[:, :, (c - c0) * P : (c - c0 + 1) * P]

        def load_gates(d0, d1, b0, b1):
            raw = sb([P, d1 - d0, (b1 - b0) * P], F32, "gates_raw%d_%d" % (d0, b0))
            nc.sync.dma_start(out=raw[:], in_=gate[d0:d1, :, b0 * P : b1 * P].rearrange("d p v -> p d v"))
            return raw

        def negate_gates(raw, d0, d1, b0, b1):
            for d in range(d0, d1):
                nc.scalar.activation(out=gates[d][:, b0 * P : b1 * P], in_=raw[:, d - d0, :], func=COPY, scale=-1.0)

        nc.gpsimd.memset(x_plane[:].bitcast(I32), 0)
        nc.gpsimd.memset(w2_raw_plane[:].bitcast(I32), 0)
        load_scales(nc.gpsimd, w2_raw_plane, w2_scales, (0, 1))
        make_identity(nc, identity[:])
        load_w1(0, 1)
        load_scales(nc.sync, x_plane, x_scales)
        load_words(x_codes, x_words)
        load_w1(1, 2)
        first = load_gates(0, 3, 0, 2)
        load_words(w2_raw, w2_words)
        load_scales(nc.sync, w2_raw_plane, w2_scales, (2, 3))
        for d, pos in enumerate((pos1, pos2, pos3)):
            nc.sync.dma_start(lists[d][:], pos)
        load_w1(2, 3)
        load_w1(3, 4)
        rest = load_gates(0, 3, 2, 4)
        nc.vector.memset(warm[:], 0.0)
        nc.scalar.activation(out=warm[:, 0:1], in_=warm[:, 1:2], func=COPY, scale=-1.0)

        h, made = [], {}

        def first_layer(c):
            grouped = sb([P, P, PACK], BF16, "w1_bf%d" % c)
            source = w1_raw[c].rearrange("p j m -> p m j")
            if c == 0:
                nc.vector.tensor_copy(out=grouped[:], in_=source)
            else:
                nc.scalar.copy(out=grouped[:], in_=source)
            codes = sb([P, P], U32, "w1_codes%d" % c)
            plane = sb([P, P], U8, "w1_plane%d" % c)
            nc.vector.quantize_mx(out=codes[:].bitcast(FP8X4), scales=plane[:], in_=grouped[:].rearrange("p m j -> p (m j)"))
            h.append(sb([P, T], F32, "h%d" % c))
            parts = 2 if c == 0 else 1
            for part in range(parts):
                cols = slice(part * T // parts, (part + 1) * T // parts)
                bank = acc_banks[(c + 2 * part) % 3]
                nc.tensor.matmul_mx(
                    out=bank[:, cols], lhsT=codes[:].bitcast(FP8X4), lhsT_scale=plane[:],
                    rhs=x_codes[:, cols].bitcast(FP8X4), rhs_scale=x_plane[:, cols], start=True, stop=True,
                )
                if part == 0:
                    nc.scalar.copy(out=h[c][:, cols], in_=bank[:, cols])
                else:
                    nc.vector.tensor_copy(out=h[c][:, cols], in_=bank[:, cols])

        def deal_w2():
            nc.vector.tensor_copy(
                out=w2_codes[:].bitcast(I32).rearrange("p (t c i) -> p c t i", t=PACK, i=4),
                in_=w2_raw[:].bitcast(I32).rearrange("p (c i t) -> p c t i", t=PACK, i=4),
            )

        def deal_w2_plane():
            nc.vector.tensor_copy(
                out=w2_plane[:].rearrange("p (t c i) -> p c t i", t=PACK, i=16),
                in_=w2_raw_plane[:].rearrange("p (c i t) -> p c t i", t=PACK, i=16),
            )

        def sum_bank(b, c):
            if b == BLOCKS - 1 and c == CHUNKS - 1:
                return sum_banks[1]
            return sum_banks[b % 3]

        def add_turned(b, c, rows, start, stop):
            nc.tensor.matmul(
                out=sum_bank(b, c)[:, c * P : (c + 1) * P], lhsT=rows, rhs=identity[:],
                is_transpose=True, start=start, stop=stop,
            )

        def gather(b0, b1, c, terms):
            for b in range(b0, b1):
                add_turned(b, c, h[c][:, b * P : (b + 1) * P], True, False)
            for d in range(D):
                offsets = lists[d][:, b0 * P // 16 : b1 * P // 16]
                nc.vector.tensor_tensor(terms[d], h[c][:].indirect(offsets), gates[d][:, b0 * P : b1 * P], MULT)
                for b in range(b0, b1):
                    add_turned(b, c, terms[d][:, (b - b0) * P : (b - b0 + 1) * P], False, d == D - 1)

        def room(count, width, name, tag=None):
            tile = sb([P, count, width], F32, name, tag)
            return [tile[:, i, :] for i in range(count)]

        z_rows = [sb([P, 2, P, 2], BF16, "z_rows%d" % b) for b in range(BLOCKS)]

        def round_z(b, c0, c1):
            rows = slice(32 * c0, 32 * c1)
            nc.scalar.copy(
                out=z_rows[b][:, :, rows, :],
                in_=sum_bank(b, c0)[:].rearrange("v (p u e) -> v u p e", u=2, e=2)[:, :, rows, :],
            )

        results = {}

        grouped_z = {}

        def turn_back(b):
            back_bank = back_banks[b % 2]
            words = z_rows[b][:].rearrange("v u p e -> v (u p e)").bitcast(F32)
            for u in range(2):
                nc.tensor.transpose(back_bank[:, u * P : (u + 1) * P], words[:, u * P : (u + 1) * P], identity[:])
            z_grouped = sb([P, P * PACK], BF16, "z_grouped%d" % b)
            nc.scalar.copy(
                out=z_grouped[:].bitcast(F32).rearrange("p (v u) -> p v u", u=2),
                in_=back_bank[:, 0 : 2 * P].rearrange("p (u v) -> p v u", u=2),
            )
            grouped_z[b] = z_grouped

        def second_layer(b):
            z_grouped = grouped_z[b]
            codes = sb([P, P], U32, "z_codes%d" % b)
            plane = sb([P, P], U8, "z_plane%d" % b)
            nc.vector.quantize_mx(out=codes[:].bitcast(FP8X4), scales=plane[:], in_=z_grouped[:])
            last = b == BLOCKS - 1
            bank = acc_banks[(b + 1) % 3]
            y = sb([P, PACK, P], F32, "y%d" % b)
            flat = y[:].rearrange("p t v -> p (t v)")
            for t in range(PACK):
                m = slice(t * P, (t + 1) * P)
                target = acc_banks[(b + 2) % 3] if last and t >= 2 else bank
                nc.tensor.matmul_mx(
                    out=target[:, m], lhsT=w2_codes[:, m].bitcast(FP8X4), lhsT_scale=w2_plane[:, m],
                    rhs=codes[:].bitcast(FP8X4), rhs_scale=plane[:], start=True, stop=True,
                )
            y_grouped = sb([P, P, PACK], BF16, "y_grouped%d" % b)
            turned = bank[:].rearrange("p (t v) -> p v t", t=PACK)
            if last:
                other = acc_banks[(b + 2) % 3]
                nc.scalar.copy(out=y_grouped[:, :, 0:2], in_=turned[:, :, 0:2])
                nc.vector.tensor_copy(out=y_grouped[:, :, 2:4], in_=other[:].rearrange("p (t v) -> p v t", t=PACK)[:, :, 2:4])
                nc.scalar.copy(out=flat[:, 0 : 2 * P], in_=bank[:, 0 : 2 * P])
                nc.scalar.copy(out=flat[:, 2 * P : 4 * P], in_=other[:, 2 * P : 4 * P])
            else:
                if b == BLOCKS - 2:
                    nc.vector.tensor_copy(out=y_grouped[:], in_=turned)
                else:
                    nc.scalar.copy(out=y_grouped[:], in_=turned)
                nc.scalar.copy(out=flat, in_=bank[:])
            rows = out_0.rearrange("(p t) v -> p t v", t=PACK)[:, :, b * P : (b + 1) * P]
            if last:
                nc.sync.dma_start(out=rows[:, 0:2, :], in_=y[:, 0:2, :])
                nc.scalar.dma_start(out=rows[:, 2:4, :], in_=y[:, 2:4, :])
            else:
                nc.sync.dma_start(out=rows, in_=y[:])
            results[b] = y_grouped

        def finish(b):
            cols = slice(b * P, (b + 1) * P)
            y_grouped = results[b]
            nc.vector.quantize_mx(
                out=y_codes[:, cols].bitcast(FP8X4), scales=y_plane[:, cols],
                in_=y_grouped[:].rearrange("p v t -> p (v t)"),
            )
            nc.sync.dma_start(
                out=out_1[0].rearrange("p n t -> p (n t)").bitcast(I32)[:, cols], in_=y_codes[:, cols].bitcast(I32)
            )

        first_layer(0)
        negate_gates(first, 0, 3, 0, 2)
        first_layer(1)
        deal_w2()
        deal_w2_plane()
        gather(0, 2, 0, room(D, 2 * P, "terms_a"))
        first_layer(2)
        gather(0, 2, 1, room(D, 2 * P, "terms_c", "w1_bf2"))
        first_layer(3)
        gather(0, 2, 2, room(D, 2 * P, "terms_d", "w1_bf3"))
        negate_gates(rest, 0, 3, 2, 4)
        gather(0, 2, 3, room(D, 2 * P, "terms_e"))
        round_z(0, 0, CHUNKS)
        round_z(1, 0, CHUNKS)
        held = room(CHUNKS * D, P, "held", "w1_bf3")
        gather(2, 3, 0, held[0:3])
        gather(2, 3, 1, held[3:6])
        turn_back(0)
        gather(2, 3, 2, held[6:9])
        turn_back(1)
        gather(2, 3, 3, held[9:12])
        second_layer(0)
        round_z(2, 0, CHUNKS)
        gather(3, 4, 0, room(D, P, "terms_f", "z_grouped0"))
        second_layer(1)
        late = room(3 * D, P, "late", "z_grouped1")
        gather(3, 4, 1, late[0:3])
        turn_back(2)
        gather(3, 4, 2, late[3:6])
        round_z(3, 0, CHUNKS - 1)
        gather(3, 4, 3, late[6:9])
        round_z(3, CHUNKS - 1, CHUNKS)
        second_layer(2)
        turn_back(3)
        finish(0)
        finish(1)
        finish(2)
        second_layer(3)
        finish(3)
        for q in range(4):
            queue = nc.scalar if q % 2 else nc.sync
            queue.dma_start(out=out_2[0, 4 * q : 4 * q + 4, :].bitcast(I32), in_=y_plane[32 * q : 32 * q + 4, :].bitcast(I32))
